import numpy as np, ml_dtypes
CORES = [3,5,43,45,51,53,67,69,75,77,83,85,91,93,115,117]
N = 16
DEG, TK, TIMES = 4, 64, 3
MASK = [[0,2,12,14],[0,1,3,13],[1,2,14,15],[2,3,7,12],[4,5,7,9],[0,5,8,15],[4,6,7,11],[2,6,7,10],[1,5,6,8],[4,9,13,14],[4,5,10,11],[8,11,12,14],[4,7,11,12],[0,4,11,13],[6,7,9,14],[1,11,14,15]]
def setup_inputs(rng):
    return {"x": rng.standard_normal((N, 128, TK), dtype=np.float32).astype(ml_dtypes.bfloat16), "w": (rng.standard_normal((N, 128, DEG * 128), dtype=np.float32) / np.float32(np.sqrt(128 * DEG / 2))).astype(ml_dtypes.bfloat16)}
def setup_inputs_big(rng):
    d = setup_inputs(rng)
    for k in ("x",): d[k] = (d[k].astype(np.float32) * 1048576.0).astype(d[k].dtype)
    return d
def setup_inputs_small(rng):
    d = setup_inputs(rng)
    for k in ("x",): d[k] = (d[k].astype(np.float32) * (1 / 1048576.0)).astype(d[k].dtype)
    return d
def setup_inputs_apart(rng):
    d = setup_inputs(rng)
    f = (10.0 ** rng.permutation(np.linspace(-1.5, 1.5, N))).astype(np.float32).reshape(N, 1, 1)
    for k in ("x",): d[k] = (d[k].astype(np.float32) * f).astype(d[k].dtype)
    return d
def reference(x, w):
    X, W = x.astype(np.float64), w.astype(np.float64)
    h = list(X)
    for _ in range(TIMES):
        h = [np.maximum(sum(W[r][:, 128 * i:128 * i + 128].T @ h[j] for i, j in enumerate(MASK[r])), 0.0) for r in range(N)]
    return {"y": np.stack(h).astype(ml_dtypes.bfloat16)}

from concourse.bass import DstId, RemoteDMATransfer
from concourse.mybir import AluOpType

N, TK, DEG, TIMES, FEAT = 16, 64, 4, 3, 128
NSIM = 128
HOP = 2.5
GUESTS_AT_RANK_CORE = True

SCRATCH = {
    "H": ("sbuf", [FEAT, TIMES * N * TK], "bfloat16"),
    "W": ("sbuf", [FEAT, 2 * DEG * FEAT], "bfloat16"),
    "Z": ("sbuf", [FEAT, TK], "float32"),
    "Y": ("sbuf", [FEAT, TK], "bfloat16"),
}
for _k in range(2 * TIMES):
    SCRATCH["ps%d" % _k] = ("psum", [FEAT, 512], "float32")

SEMAPHORES = (["ldw", "wa", "zs", "st", "sent"]
              + ["a%d_%d" % (t, j) for t in range(TIMES + 1) for j in range(N)]
              + ["m%d" % k for k in range(2 * TIMES)])


def _bits(m):
    return bin(m).count("1")


def make_plan(cores, M, topo):
    n = len(cores)

    def is_open(c):
        return all(topo.may_write(c, d) for d in cores if d != c)

    host, relay = [], []
    for c in cores:
        if is_open(c):
            host.append(c)
            relay.append(c)
            continue
        here = [d for d in range(NSIM) if topo.chip(d) == topo.chip(c) and is_open(d)]
        pals = [d for d in here if d in cores]
        spare = [d for d in here if d not in cores and topo.die(d) == topo.die(c)]
        relay.append(pals[0] if pals else spare[0])
        host.append(pals[0] if (pals and GUESTS_AT_RANK_CORE) else spare[0])

    def site(t, r):
        return cores[r] if t in (0, TIMES) else host[r]

    wants = []
    for t in range(TIMES):
        w = {}
        for r in range(n):
            w.setdefault(site(t + 1, r), set()).update(M[r])
        wants.append(w)

    sends = [{} for _ in range(TIMES)]
    fwd = {}
    for t in range(TIMES):
        for q in sorted(wants[t]):
            for j in sorted(wants[t][q]):
                s = site(t, j)
                if s == q:
                    continue
                if topo.may_write(s, q):
                    sends[t].setdefault(s, {}).setdefault(q, []).append(j)
                else:
                    fwd.setdefault(relay[j], {}).setdefault(q, []).append(j)
    for s in sorted(fwd):
        for j in sorted(set(j for js in fwd[s].values() for j in js)):
            got = sends[0].setdefault(cores[j], {}).setdefault(s, [])
            if j not in got:
                got.append(j)

    def items_of(dm):
        out = []
        for q in sorted(dm):
            run = []
            for j in sorted(dm[q]):
                if run and j != run[-1] + 1:
                    out.append((q, tuple(run)))
                    run = []
                run.append(j)
            out.append((q, tuple(run)))
        return out

    R = {TIMES: {}}
    order = {}
    for t in range(TIMES - 1, -1, -1):
        R[t] = {}
        for s in sorted(sends[t]):
            its = items_of(sends[t][s])
            urgent = set(q for q, run in its if t == 0 and any(j in js for js in fwd.get(q, {}).values() for j in run))
            its.sort(key=lambda it: (0 if it[0] in urgent else 1, -R[t + 1].get(it[0], 0.0),
                                     0 if topo.chip(it[0]) != topo.chip(s) else 1, len(it[1]), it[1], it[0]))
            order[(t, s)] = its
            R[t][s] = max(k + 1 + HOP + R[t + 1].get(q, 0.0) for k, (q, _) in enumerate(its))
    forder = {}
    for s in sorted(fwd):
        its = items_of(fwd[s])
        its.sort(key=lambda it: (-R[1].get(it[0], 0.0), it[1], it[0]))
        forder[s] = its
    return dict(host=host, relay=relay, site=site, wants=wants, order=order, forder=forder, R=R)


def rank_program(g, core, T, topo):
    cores, M = list(T.cores), T.tables["MASK"]
    plan = make_plan(cores, M, topo)
    host, site, order, forder = plan["host"], plan["site"], plan["order"], plan["forder"]
    rank = T.rank_of(core)
    hosted = [[r for r in range(N) if site(t, r) == core] for t in range(TIMES + 1)]
    if rank is None and not any(hosted):
        return

    def cols(t, j0, j1=None):
        j1 = j0 if j1 is None else j1
        return T.H[:, (t * N + j0) * TK:(t * N + j1 + 1) * TK]

    def mask_for(src, q):
        if topo.chip(q) != topo.chip(src):
            return topo.mask(src, q)
        far = [d for d in range(NSIM) if topo.chip(d) != topo.chip(src)][0]
        return (topo.mask(src, q) & ~topo.mask(src, far)) or topo.mask(src, q)

    here = {}
    for (t, s), its in list(order.items()) + [((0, s), its) for s, its in forder.items()]:
        for q, run in its:
            if q == core:
                for j in run:
                    here[(t, j)] = ("a%d_%d" % (t, run[0]), _bits(mask_for(s, q)))
    if rank is not None:
        here[(0, rank)] = ("a0_%d" % rank, 16)
    for t in range(1, TIMES + 1):
        for r in hosted[t]:
            here[(t, r)] = ("a%d_%d" % (t, r), 1)

    seen = {}

    def wait(queue, name, sem_cnt):
        if (name, sem_cnt[0]) not in seen:
            seen[(name, sem_cnt[0])] = True
            queue.wait_ge(T.sem[sem_cnt[0]], sem_cnt[1])

    if rank is not None:
        g.sync.dma_start(cols(0, rank), T.x[:]).then_inc(T.sem[here[(0, rank)][0]], 16)
        g.scalar.dma_start(T.W[:, 0:DEG * FEAT], T.w[:]).then_inc(T.sem.ldw, 16)
    g.vector.memset(T.Z[:], 0.0).then_inc(T.sem.zs, 1)
    g.vector.wait_ge(T.sem.zs, 1)

    sent = [0]

    def send(t, its):
        i = 0
        while i < len(its):
            k = i
            m = mask_for(core, its[i][0])
            while k < len(its) and its[k][1] == its[i][1] and mask_for(core, its[k][0]) == m:
                k += 1
            run = its[i][1]
            for j in run:
                wait(g, "g", here[(t, j)])
            ids = []
            for q, _ in its[i:k]:
                rid, pid, _se = topo.addr(q)
                ids.append(DstId(rid=rid, pnc=pid))
            ap = cols(t, run[0], run[-1])
            g.remote_dma_fused([RemoteDMATransfer(dst_ids=ids, dma_engine_mask=m, remote_sem=T.sem["a%d_%d" % (t, run[0])],
                                                  srcs=[ap], dsts=[ap for _ in ids], alu_op=0)], local_sem=T.sem.sent)
            sent[0] += _bits(m)
            i = k

    send(0, order.get((0, core), []))
    if rank is not None and host[rank] != core:
        wait(g, "g", ("ldw", 16))
        rid, pid, _se = topo.addr(host[rank])
        m = mask_for(core, host[rank])
        g.remote_dma(T.W[:, DEG * FEAT:2 * DEG * FEAT], T.W[:, 0:DEG * FEAT], T.sem.wa, T.sem.sent, pid, rid, m)
        sent[0] += _bits(m)
    send(0, forder.get(core, []))

    def comp_order(t):
        first = []
        for _q, run in order.get((t, core), []):
            for j in run:
                if j not in first:
                    first.append(j)
        return first + [r for r in hosted[t] if r not in first]

    bank = 0
    for t in range(1, TIMES + 1):
        for r in comp_order(t):
            ps = T["ps%d" % bank]
            msem = T.sem["m%d" % bank]
            bank += 1
            if cores[r] == core:
                wait(g.tensor, "t", ("ldw", 16))
                w0 = 0
            else:
                wait(g.tensor, "t", ("wa", _bits(mask_for(cores[r], core))))
                w0 = DEG * FEAT

            def late(i):
                j = M[r][i]
                s = site(t - 1, j)
                if s == core:
                    return (0, 0, i)
                if not topo.may_write(s, core):
                    return (3, 0, i)
                pos = [k for k, it in enumerate(order[(t - 1, s)]) if it[0] == core and j in it[1]][0]
                return (1, pos, i)
            seq = sorted(range(DEG), key=late)
            mm = None
            for n_, i in enumerate(seq):
                j = M[r][i]
                wait(g.tensor, "t", here[(t - 1, j)])
                mm = g.tensor.matmul(ps[:, 0:TK], T.W[:, w0 + i * FEAT:w0 + (i + 1) * FEAT], cols(t - 1, j),
                                     start=(n_ == 0), stop=(n_ == DEG - 1))
            mm.then_inc(msem, 1)
            g.vector.wait_ge(msem, 1)
            out = T.Y[:] if t == TIMES else cols(t, r)
            g.vector.tensor_tensor(out=out, in0=ps[:, 0:TK], in1=T.Z[:], op=AluOpType.max).then_inc(T.sem[here[(t, r)][0]], 1)
        if t < TIMES:
            send(t, order.get((t, core), []))

    if rank is not None:
        g.sync.wait_ge(T.sem[here[(TIMES, rank)][0]], 1)
        g.sync.dma_start(T.y[:], T.Y[:]).then_inc(T.sem.st, 16)
        g.sync.wait_ge(T.sem.st, 16)
    if sent[0]:
        g.wait_ge(T.sem.sent, sent[0])
